import numpy as np, ml_dtypes
CORES = [3,11,19,27,35,43,51,59]
N = 8
def setup_inputs(rng):
    return {"x": rng.standard_normal((N, 128, 64), dtype=np.float32).astype(ml_dtypes.bfloat16)}
def reference(x):
    g = np.ascontiguousarray(x.transpose(1, 2, 0)).reshape(128, 64 * N)
    return {"y": np.broadcast_to(g, (N,) + g.shape)}

@@ -1,0 +1,44 @@
+import concourse.bass as bass
+
+N = 8
+SCRATCH = {
+    "xd": ("dram", [N, 128, 8], "bfloat16"),
+    "h": ("sbuf", [128, N, 8], "bfloat16"),
+    "m": ("sbuf", [128, 8, N], "bfloat16"),
+    "gth": ("dram", [N, 128, 64], "bfloat16"),
+}
+SEMAPHORES = ["ld", "mix", "st", "s1", "s3", "sent"]
+
+
+def rank_program(g, core, T, topo):
+    r = T.rank_of(core)
+    if r is None:
+        return
+    S = T.sem
+
+    def dst(c):
+        a = topo.addr(c)
+        return bass.DstId(rid=a[0], pnc=a[1])
+
+    others = [k for k in range(N) if k != r]
+    g.dma_start(T.xd[:], T.x[:]).then_inc(S.ld, 16)
+    g.wait_ge(S.ld, 16)
+    g.remote_dma_fused(
+        [bass.RemoteDMATransfer(dst_ids=[dst(T.cores[k])], dma_engine_mask=1 << i, remote_sem=S.s1,
+                                src=T.xd[k], dst=T.h[:, r, :]) for i, k in enumerate(others)],
+        local_sem=S.sent)
+    g.dma_start(T.m[:, :, r:r + 1], T.x[16 * r:16 * r + 16, :], allow_slow_non_contiguous=True).then_inc(S.mix, 16)
+    g.wait_ge(S.s1, N - 1)
+    for k in others:
+        g.dma_start(T.m[:, :, k:k + 1], T.h[:, k, :], allow_slow_non_contiguous=True).then_inc(S.mix, 16)
+    g.wait_ge(S.mix, 16 * N)
+    g.remote_dma_fused(
+        [bass.RemoteDMATransfer(dst_ids=[dst(T.cores[k]) for k in others], dma_engine_mask=0xFF, remote_sem=S.s3,
+                                srcs=[T.m[:]], dsts=[T.gth[r] for k in others])],
+        local_sem=S.sent)
+    g.dma_start(T.gth[r], T.m[:]).then_inc(S.st, 16)
+    g.wait_ge(S.st, 16)
+    g.wait_ge(S.s3, 8 * (N - 1))
+    g.dma_start(T.y[:], T.gth[:]).then_inc(S.st, 16)
+    g.wait_ge(S.st, 32)
+    g.wait_ge(S.sent, (N - 1) + 8)

@@ -3,35 +3,47 @@ import concourse.bass as bass
 N = 8
 SCRATCH = {
     "xd": ("dram", [N, 128, 8], "bfloat16"),
-    "h": ("sbuf", [128, N, 8], "bfloat16"),
+    "h": ("sbuf", [128, 8], "bfloat16"),
     "m": ("sbuf", [128, 8, N], "bfloat16"),
     "gth": ("dram", [N, 128, 64], "bfloat16"),
 }
-SEMAPHORES = ["ld", "mix", "st", "s1", "s3", "sent"]
+SEMAPHORES = ["ld", "mix", "st", "s1", "s2", "s3", "sent"]
+HELPERS = [0, 1, 2, 4, 5, 6, 7]
 
 
 def rank_program(g, core, T, topo):
-    r = T.rank_of(core)
-    if r is None:
-        return
     S = T.sem
+    chip, loc = core // 8, core % 8
 
     def dst(c):
         a = topo.addr(c)
         return bass.DstId(rid=a[0], pnc=a[1])
 
+    def helper(k, r):
+        return 8 * k + HELPERS[r if r < k else r - 1]
+
+    r = T.rank_of(core)
+    if r is None:
+        i = HELPERS.index(loc)
+        src = i if i < chip else i + 1
+        g.wait_ge(S.s1, 1)
+        g.remote_dma_fused(
+            [bass.RemoteDMATransfer(dst_ids=[dst(T.cores[chip])], dma_engine_mask=3 << (2 * s), remote_sem=S.s2,
+                                    src=T.h[:, s:s + 1], dst=T.m[:, s, src:src + 1]) for s in range(8)],
+            local_sem=S.sent)
+        g.wait_ge(S.sent, 16)
+        return
+
     others = [k for k in range(N) if k != r]
     g.dma_start(T.xd[:], T.x[:]).then_inc(S.ld, 16)
     g.wait_ge(S.ld, 16)
     g.remote_dma_fused(
-        [bass.RemoteDMATransfer(dst_ids=[dst(T.cores[k])], dma_engine_mask=1 << i, remote_sem=S.s1,
-                                src=T.xd[k], dst=T.h[:, r, :]) for i, k in enumerate(others)],
+        [bass.RemoteDMATransfer(dst_ids=[dst(helper(k, r))], dma_engine_mask=1 << i, remote_sem=S.s1,
+                                src=T.xd[k], dst=T.h[:]) for i, k in enumerate(others)],
         local_sem=S.sent)
     g.dma_start(T.m[:, :, r:r + 1], T.x[16 * r:16 * r + 16, :], allow_slow_non_contiguous=True).then_inc(S.mix, 16)
-    g.wait_ge(S.s1, N - 1)
-    for k in others:
-        g.dma_start(T.m[:, :, k:k + 1], T.h[:, k, :], allow_slow_non_contiguous=True).then_inc(S.mix, 16)
-    g.wait_ge(S.mix, 16 * N)
+    g.wait_ge(S.mix, 16)
+    g.wait_ge(S.s2, 16 * (N - 1))
     g.remote_dma_fused(
         [bass.RemoteDMATransfer(dst_ids=[dst(T.cores[k]) for k in others], dma_engine_mask=0xFF, remote_sem=S.s3,
                                 srcs=[T.m[:]], dsts=[T.gth[r] for k in others])],

@@ -1,11 +1,12 @@
 import concourse.bass as bass
 
 N = 8
+MC = [3, 7]
+W = 8 // len(MC)
 SCRATCH = {
-    "xd": ("dram", [N, 128, 8], "bfloat16"),
+    "xs": ("sbuf", [128, 64], "bfloat16"),
     "h": ("sbuf", [128, 8], "bfloat16"),
-    "m": ("sbuf", [128, 8, N], "bfloat16"),
-    "gth": ("dram", [N, 128, 64], "bfloat16"),
+    "yy": ("sbuf", [128, 64, N], "bfloat16"),
 }
 SEMAPHORES = ["ld", "mix", "st", "s1", "s2", "s3", "sent"]
 HELPERS = [0, 1, 2, 4, 5, 6, 7]
@@ -14,43 +15,56 @@ HELPERS = [0, 1, 2, 4, 5, 6, 7]
 def rank_program(g, core, T, topo):
     S = T.sem
     chip, loc = core // 8, core % 8
+    r = T.rank_of(core)
+    others = [k for k in range(N) if k != chip]
+    sent = 0
 
     def dst(c):
         a = topo.addr(c)
         return bass.DstId(rid=a[0], pnc=a[1])
 
-    def helper(k, r):
-        return 8 * k + HELPERS[r if r < k else r - 1]
+    def helper(k, q):
+        return 8 * k + HELPERS[q if q < k else q - 1]
 
-    r = T.rank_of(core)
-    if r is None:
-        i = HELPERS.index(loc)
-        src = i if i < chip else i + 1
-        g.wait_ge(S.s1, 1)
+    if r is not None:
+        g.dma_start(T.xs[:], T.x[:]).then_inc(S.ld, 16)
+        g.wait_ge(S.ld, 16)
         g.remote_dma_fused(
-            [bass.RemoteDMATransfer(dst_ids=[dst(T.cores[chip])], dma_engine_mask=3 << (2 * s), remote_sem=S.s2,
-                                    src=T.h[:, s:s + 1], dst=T.m[:, s, src:src + 1]) for s in range(8)],
+            [bass.RemoteDMATransfer(dst_ids=[dst(helper(k, r))], dma_engine_mask=1 << i, remote_sem=S.s1,
+                                    src=T.xs[:, 8 * k:8 * k + 8], dst=T.h[:]) for i, k in enumerate(others)],
             local_sem=S.sent)
-        g.wait_ge(S.sent, 16)
-        return
+        sent += N - 1
+        src, buf, off = r, T.xs, 8 * r
+    else:
+        i = HELPERS.index(loc)
+        src, buf, off = (i if i < chip else i + 1), T.h, 0
+        g.wait_ge(S.s1, 1)
 
-    others = [k for k in range(N) if k != r]
-    g.dma_start(T.xd[:], T.x[:]).then_inc(S.ld, 16)
-    g.wait_ge(S.ld, 16)
-    g.remote_dma_fused(
-        [bass.RemoteDMATransfer(dst_ids=[dst(helper(k, r))], dma_engine_mask=1 << i, remote_sem=S.s1,
-                                src=T.xd[k], dst=T.h[:]) for i, k in enumerate(others)],
-        local_sem=S.sent)
-    g.dma_start(T.m[:, :, r:r + 1], T.x[16 * r:16 * r + 16, :], allow_slow_non_contiguous=True).then_inc(S.mix, 16)
-    g.wait_ge(S.mix, 16)
-    g.wait_ge(S.s2, 16 * (N - 1))
-    g.remote_dma_fused(
-        [bass.RemoteDMATransfer(dst_ids=[dst(T.cores[k]) for k in others], dma_engine_mask=0xFF, remote_sem=S.s3,
-                                srcs=[T.m[:]], dsts=[T.gth[r] for k in others])],
-        local_sem=S.sent)
-    g.dma_start(T.gth[r], T.m[:]).then_inc(S.st, 16)
-    g.wait_ge(S.st, 16)
-    g.wait_ge(S.s3, 8 * (N - 1))
-    g.dma_start(T.y[:], T.gth[:]).then_inc(S.st, 16)
-    g.wait_ge(S.st, 32)
-    g.wait_ge(S.sent, (N - 1) + 8)
+    tr = [bass.RemoteDMATransfer(dst_ids=[dst(8 * chip + MC[jl // W])], dma_engine_mask=3 << (2 * jl), remote_sem=S.s2,
+                                 src=buf[:, off + jl:off + jl + 1], dst=T.yy[:, 8 * chip + jl, src:src + 1])
+          for jl in range(8) if MC[jl // W] != loc]
+    g.remote_dma_fused(tr, local_sem=S.sent)
+    sent += 2 * len(tr)
+
+    if loc in MC:
+        b = MC.index(loc) * W
+        j0 = 8 * chip + b
+        g.dma_start(T.yy[:, j0:j0 + W, src:src + 1], buf[:, off + b:off + b + W],
+                    allow_slow_non_contiguous=True).then_inc(S.mix, 16)
+        g.wait_ge(S.mix, 16)
+        g.wait_ge(S.s2, 2 * W * (N - 1))
+        blk = T.yy[:, j0:j0 + W, :]
+        tr = [bass.RemoteDMATransfer(dst_ids=[dst(T.cores[k]) for k in others], dma_engine_mask=0x00FF,
+                                     remote_sem=S.s3, srcs=[blk], dsts=[blk for k in others])]
+        sent += 8
+        if r is None:
+            tr.append(bass.RemoteDMATransfer(dst_ids=[dst(T.cores[chip])], dma_engine_mask=0xFF00,
+                                             remote_sem=S.s3, srcs=[blk], dsts=[blk]))
+            sent += 8
+        g.remote_dma_fused(tr, local_sem=S.sent)
+
+    if r is not None:
+        g.wait_ge(S.s3, 8 * (N * len(MC) - 1))
+        g.dma_start(T.y[:], T.yy[:]).then_inc(S.st, 16)
+        g.wait_ge(S.st, 16)
+    g.wait_ge(S.sent, sent)

@@ -9,35 +9,32 @@ SCRATCH = {
     "yy": ("sbuf", [128, 64, N], "bfloat16"),
 }
 SEMAPHORES = ["ld", "mix", "st", "s1", "s2", "s3", "sent"]
-HELPERS = [0, 1, 2, 4, 5, 6, 7]
+HELPER = {1: 7, 2: 2, 4: 6, 6: 0, 3: 1, 5: 4, 7: 5}
+FAR_FIRST = [3, 5, 7, 2, 4, 6, 1]
 
 
 def rank_program(g, core, T, topo):
     S = T.sem
     chip, loc = core // 8, core % 8
     r = T.rank_of(core)
-    others = [k for k in range(N) if k != chip]
     sent = 0
 
     def dst(c):
         a = topo.addr(c)
         return bass.DstId(rid=a[0], pnc=a[1])
 
-    def helper(k, q):
-        return 8 * k + HELPERS[q if q < k else q - 1]
-
     if r is not None:
         g.dma_start(T.xs[:], T.x[:]).then_inc(S.ld, 16)
         g.wait_ge(S.ld, 16)
         g.remote_dma_fused(
-            [bass.RemoteDMATransfer(dst_ids=[dst(helper(k, r))], dma_engine_mask=1 << i, remote_sem=S.s1,
-                                    src=T.xs[:, 8 * k:8 * k + 8], dst=T.h[:]) for i, k in enumerate(others)],
+            [bass.RemoteDMATransfer(dst_ids=[dst(8 * (r ^ m) + HELPER[m])], dma_engine_mask=1 << i, remote_sem=S.s1,
+                                    src=T.xs[:, 8 * (r ^ m):8 * (r ^ m) + 8], dst=T.h[:])
+             for i, m in enumerate(FAR_FIRST)],
             local_sem=S.sent)
         sent += N - 1
         src, buf, off = r, T.xs, 8 * r
     else:
-        i = HELPERS.index(loc)
-        src, buf, off = (i if i < chip else i + 1), T.h, 0
+        src, buf, off = chip ^ [m for m in HELPER if HELPER[m] == loc][0], T.h, 0
         g.wait_ge(S.s1, 1)
 
     tr = [bass.RemoteDMATransfer(dst_ids=[dst(8 * chip + MC[jl // W])], dma_engine_mask=3 << (2 * jl), remote_sem=S.s2,
@@ -54,8 +51,8 @@ def rank_program(g, core, T, topo):
         g.wait_ge(S.mix, 16)
         g.wait_ge(S.s2, 2 * W * (N - 1))
         blk = T.yy[:, j0:j0 + W, :]
-        tr = [bass.RemoteDMATransfer(dst_ids=[dst(T.cores[k]) for k in others], dma_engine_mask=0x00FF,
-                                     remote_sem=S.s3, srcs=[blk], dsts=[blk for k in others])]
+        tr = [bass.RemoteDMATransfer(dst_ids=[dst(T.cores[chip ^ m]) for m in FAR_FIRST], dma_engine_mask=0x00FF,
+                                     remote_sem=S.s3, srcs=[blk], dsts=[blk for m in FAR_FIRST])]
         sent += 8
         if r is None:
             tr.append(bass.RemoteDMATransfer(dst_ids=[dst(T.cores[chip])], dma_engine_mask=0xFF00,

@@ -10,6 +10,7 @@ SCRATCH = {
 }
 SEMAPHORES = ["ld", "mix", "st", "s1", "s2", "s3", "sent"]
 HELPER = {1: 7, 2: 2, 4: 6, 6: 0, 3: 1, 5: 4, 7: 5}
+SLICES = [1, 3, 5, 7, 2, 4, 6]
 FAR_FIRST = [3, 5, 7, 2, 4, 6, 1]
 
 
@@ -29,7 +30,7 @@ def rank_program(g, core, T, topo):
         g.remote_dma_fused(
             [bass.RemoteDMATransfer(dst_ids=[dst(8 * (r ^ m) + HELPER[m])], dma_engine_mask=1 << i, remote_sem=S.s1,
                                     src=T.xs[:, 8 * (r ^ m):8 * (r ^ m) + 8], dst=T.h[:])
-             for i, m in enumerate(FAR_FIRST)],
+             for i, m in enumerate(SLICES)],
             local_sem=S.sent)
         sent += N - 1
         src, buf, off = r, T.xs, 8 * r
@@ -37,6 +38,11 @@ def rank_program(g, core, T, topo):
         src, buf, off = chip ^ [m for m in HELPER if HELPER[m] == loc][0], T.h, 0
         g.wait_ge(S.s1, 1)
 
+    if loc in MC:
+        b = MC.index(loc) * W
+        j0 = 8 * chip + b
+        g.dma_start(T.yy[:, j0:j0 + W, src:src + 1], buf[:, off + b:off + b + W],
+                    allow_slow_non_contiguous=True).then_inc(S.mix, 16)
     tr = [bass.RemoteDMATransfer(dst_ids=[dst(8 * chip + MC[jl // W])], dma_engine_mask=3 << (2 * jl), remote_sem=S.s2,
                                  src=buf[:, off + jl:off + jl + 1], dst=T.yy[:, 8 * chip + jl, src:src + 1])
           for jl in range(8) if MC[jl // W] != loc]
@@ -44,10 +50,6 @@ def rank_program(g, core, T, topo):
     sent += 2 * len(tr)
 
     if loc in MC:
-        b = MC.index(loc) * W
-        j0 = 8 * chip + b
-        g.dma_start(T.yy[:, j0:j0 + W, src:src + 1], buf[:, off + b:off + b + W],
-                    allow_slow_non_contiguous=True).then_inc(S.mix, 16)
         g.wait_ge(S.mix, 16)
         g.wait_ge(S.s2, 2 * W * (N - 1))
         blk = T.yy[:, j0:j0 + W, :]

import concourse.bass as bass

N = 8
MC = [3, 7]
W = 8 // len(MC)
SCRATCH = {
    "xs": ("sbuf", [128, 64], "bfloat16"),
    "h": ("sbuf", [128, 8], "bfloat16"),
    "yy": ("sbuf", [128, 64, N], "bfloat16"),
}
SEMAPHORES = ["ld", "mix", "st", "s1", "s2", "s3", "sent"]
HELPER = {1: 7, 2: 2, 4: 6, 6: 0, 3: 1, 5: 4, 7: 5}
SLICES = [1, 3, 5, 7, 2, 4, 6]
FAR_FIRST = [3, 5, 7, 2, 4, 6, 1]


def rank_program(g, core, T, topo):
    S = T.sem
    chip, loc = core // 8, core % 8
    r = T.rank_of(core)
    sent = 0

    def dst(c):
        a = topo.addr(c)
        return bass.DstId(rid=a[0], pnc=a[1])

    if r is not None:
        g.dma_start(T.xs[:], T.x[:]).then_inc(S.ld, 16)
        g.wait_ge(S.ld, 16)
        g.remote_dma_fused(
            [bass.RemoteDMATransfer(dst_ids=[dst(8 * (r ^ m) + HELPER[m])], dma_engine_mask=1 << i, remote_sem=S.s1,
                                    src=T.xs[:, 8 * (r ^ m):8 * (r ^ m) + 8], dst=T.h[:])
             for i, m in enumerate(SLICES)],
            local_sem=S.sent)
        sent += N - 1
        src, buf, off = r, T.xs, 8 * r
    else:
        src, buf, off = chip ^ [m for m in HELPER if HELPER[m] == loc][0], T.h, 0
        g.wait_ge(S.s1, 1)

    if loc in MC:
        b = MC.index(loc) * W
        j0 = 8 * chip + b
        g.dma_start(T.yy[:, j0:j0 + W, src:src + 1], buf[:, off + b:off + b + W],
                    allow_slow_non_contiguous=True).then_inc(S.mix, 16)
    tr = [bass.RemoteDMATransfer(dst_ids=[dst(8 * chip + MC[jl // W])], dma_engine_mask=3 << (2 * jl), remote_sem=S.s2,
                                 src=buf[:, off + jl:off + jl + 1], dst=T.yy[:, 8 * chip + jl, src:src + 1])
          for jl in range(8) if MC[jl // W] != loc]
    g.remote_dma_fused(tr, local_sem=S.sent)
    sent += 2 * len(tr)

    if loc in MC:
        g.wait_ge(S.mix, 16)
        g.wait_ge(S.s2, 2 * W * (N - 1))
        blk = T.yy[:, j0:j0 + W, :]
        tr = [bass.RemoteDMATransfer(dst_ids=[dst(T.cores[chip ^ m]) for m in FAR_FIRST], dma_engine_mask=0x00FF,
                                     remote_sem=S.s3, srcs=[blk], dsts=[blk for m in FAR_FIRST])]
        sent += 8
        if r is None:
            tr.append(bass.RemoteDMATransfer(dst_ids=[dst(T.cores[chip])], dma_engine_mask=0xFF00,
                                             remote_sem=S.s3, srcs=[blk], dsts=[blk]))
            sent += 8
        g.remote_dma_fused(tr, local_sem=S.sent)

    if r is not None:
        g.wait_ge(S.s3, 8 * (N * len(MC) - 1))
        g.dma_start(T.y[:], T.yy[:]).then_inc(S.st, 16)
        g.wait_ge(S.st, 16)
    g.wait_ge(S.sent, sent)
